import numpy as np
import ml_dtypes


def mxq(x, axis, fmt="e4m3"):
    dtype, down = {"e4m3": (ml_dtypes.float8_e4m3fn, 7), "e5m2": (ml_dtypes.float8_e5m2, 14)}[fmt]
    v = np.moveaxis(np.asarray(x, np.float32).astype(ml_dtypes.bfloat16).astype(np.float64), axis, -1)
    blocks = v.reshape(v.shape[:-1] + (-1, 32))
    amax = np.abs(blocks).max(-1, keepdims=True)
    byte = np.maximum(np.where(amax > 0, np.frexp(amax)[1] - 1 + 127, 0) - down, 1)
    scale = np.exp2(byte - 127.0)
    codes = (blocks / scale).astype(np.float32).astype(dtype).astype(np.float64)
    return np.moveaxis((codes * scale).reshape(v.shape), -1, axis)


WIDE = False


def mx_kscale(k):
    if not WIDE:
        return np.ones(k)
    levels = np.array([10, -10, 5, -5, 0])
    if k % 512:
        return np.exp2(np.random.permutation(np.resize(levels, k // 32))).repeat(32)
    a = np.empty((k // 512, 16))
    for p in range(k // 512):
        a[p, :8] = np.random.permutation(np.resize(levels, 8))
        for g in range(8):
            far = levels[np.abs(levels - a[p, g]) >= 10]
            a[p, g + 8] = far[np.random.randint(len(far))]
    return np.exp2(a.ravel()).repeat(32)


def f64(x):
    return np.asarray(x).astype(np.float64)


def striped(idx):
    return np.tile(np.asarray(idx).reshape(-1, 16).T, (8, 1)).astype(np.uint16)


def unstriped(offs):
    return offs[:16].T.reshape(-1).astype(np.int64)


B, N, T, D, DV, NQ = 1, 1024, 4096, 512, 256, 128


def setup_inputs():
    n = np.random.standard_normal
    idx = np.sort(np.random.permutation(T)[:B * N].reshape(B, N), axis=1).reshape(-1)
    s = mx_kscale(D)[:, None]
    u = np.ones(T)
    u[idx] = mx_kscale(B * N)
    r = np.random.uniform(0.5, 2.0, T)
    k = n((D, T)) / s
    v = n((DV, T)) / (u * r)
    when = np.zeros(T)
    when[idx] = np.sort(np.random.permutation(2 * N)[:B * N])
    return {
        "qT": (n((B, D, NQ)) * s * (0.60 / np.sqrt(D))).astype(np.float32),
        "kT": k.astype(np.float32),
        "vT": v.astype(np.float32),
        "vs": np.tile(u * r, (128, 1)).astype(np.float32),
        "pos": np.tile(when, (128, 1)).astype(np.float32),
        "slope": np.exp2(-np.random.randint(8, 13, (B, NQ, 1))).astype(np.float32),
        "og": n((B, NQ, DV)).astype(np.float32),
        "offs": striped(idx),
    }


def reference(qT, kT, vT, vs, pos, slope, og, offs):
    idx = unstriped(offs)
    k = f64(kT)
    v = f64(vT)
    pick = lambda x: x[:, idx].reshape(x.shape[0], B, N).transpose(1, 0, 2)
    q = f64(qT)
    score = mxq(q, 1, "e4m3").transpose(0, 2, 1) @ mxq(pick(k), 1, "e4m3")
    score = score + f64(slope) * pick(f64(pos))[:, :1, :]
    m = score.max(-1, keepdims=True)
    p = np.exp(score - m)
    total = p.sum(-1, keepdims=True)
    w = p * pick(f64(vs))[:, :1, :]
    y = mxq(w, 2, "e4m3") @ mxq(pick(v).transpose(0, 2, 1), 1, "e4m3")
    y = y / total
    y = y / (1.0 + np.exp(-f64(og)))
    return y

@@ -1,0 +1,224 @@
+from contextlib import ExitStack
+
+import concourse.mybir as mybir
+from concourse.masks import make_identity
+
+F32 = mybir.dt.float32
+BF16 = mybir.dt.bfloat16
+U32 = mybir.dt.uint32
+U16 = mybir.dt.uint16
+U8 = mybir.dt.uint8
+FP8X4 = mybir.dt.float8_e4m3fn_x4
+ACT = mybir.ActivationFunctionType
+ALU = mybir.AluOpType
+AX = mybir.AxisListType
+
+P = 128
+D = 512
+DV = 256
+T = 4096
+N = 1024
+HALF = 512
+FIRST = T - HALF
+FLOPS = 2 * N * D * P + 2 * N * P * DV
+BYTES = 4 * (D * P + D * T + DV * T + 2 * T + P + 2 * P * DV) + 2 * P * (N // 16)
+
+
+def tile_attend_x_alibi_gate_srt_kernel(tc, qT, kT, vT, vs, pos, slope, og, offs, out):
+    nc = tc.nc
+    with ExitStack() as ctx:
+        keep = ctx.enter_context(tc.tile_pool(name="keep", bufs=1))
+        banks = ctx.enter_context(tc.psum_pool(name="banks", bufs=1))
+
+        offsets = keep.tile([P, N // 16], U16, name="offsets")
+        nc.sync.dma_start(offsets[:], offs)
+
+        pos_row = keep.tile([P, T], F32, name="pos_row")
+        vs_row = keep.tile([P, T], F32, name="vs_row")
+        kp = [keep.tile([P, T], F32, name=f"k_plane{t}") for t in range(4)]
+        vp = [keep.tile([P, T], F32, name=f"v_plane{e}") for e in range(2)]
+        k_planes = kT.rearrange("(p t) n -> p t n", t=4)
+
+        nc.vector.memset(pos_row[:], 0.0)
+        nc.gpsimd.memset(vs_row[:], 0.0)
+        nc.vector.memset(kp[0][:, T // 2 : T // 2 + 8], 0.0)
+        for plane in (kp[1], kp[2], kp[3], vp[0], vp[1]):
+            nc.gpsimd.memset(plane[:, 0:8], 0.0)
+        ident = keep.tile([P, P], F32, name="ident")
+        make_identity(nc, ident[:])
+        ident_b = keep.tile([P, P], BF16, name="ident_b")
+        make_identity(nc, ident_b[:])
+
+        q_raw = keep.tile([P, 4, P], F32, name="q_raw")
+        nc.scalar.dma_start(q_raw[:], qT[0].rearrange("(p t) q -> p t q", t=4))
+        og_sb = keep.tile([P, DV], F32, name="og_sb")
+        nc.scalar.dma_start(og_sb[:], og[0])
+        slope_sb = keep.tile([P, 1], F32, name="slope_sb")
+        nc.scalar.dma_start(slope_sb[:], slope[0])
+        nc.sync.dma_start(kp[0][:, : T // 2], k_planes[:, 0, : T // 2])
+        nc.sync.dma_start(pos_row[0:1, :], pos[0:1, :])
+        nc.sync.dma_start(kp[0][:, T // 2 :], k_planes[:, 0, T // 2 :])
+        nc.sync.dma_start(vs_row[0:1, :], vs[0:1, :])
+        for t in range(1, 4):
+            if t < 3:
+                nc.sync.dma_start(kp[t][:], k_planes[:, t, :])
+            else:
+                nc.sync.dma_start(kp[t][:, :FIRST], k_planes[:, t, :FIRST])
+                nc.sync.dma_start(kp[t][:, FIRST:], k_planes[:, t, FIRST:])
+        nc.sync.dma_start(vp[0][:], vT[0:P, :])
+        nc.sync.dma_start(vp[1][:, :FIRST], vT[P : 2 * P, :FIRST])
+        nc.sync.dma_start(vp[1][:, FIRST:], vT[P : 2 * P, FIRST:])
+
+        gate = keep.tile([P, DV], F32, name="gate")
+        nc.scalar.activation(gate[:], og_sb[:], ACT.Sigmoid)
+        warm = keep.tile([P, 1], F32, name="warm")
+        nc.scalar.activation(warm[:], slope_sb[:], ACT.Exp)
+
+        q_grp = keep.tile([P, P, 4], BF16, name="q_grp", align_bytes=64)
+        nc.scalar.copy(q_grp[:], q_raw[:].rearrange("p t q -> p q t"))
+        q_codes = keep.tile([P, P], U32, name="q_codes", align_bytes=64)
+        q_scales = keep.tile([P, P], U8, name="q_scales", align_bytes=64)
+        nc.vector.quantize_mx(
+            out=q_codes[:].bitcast(FP8X4),
+            scales=q_scales[:],
+            in_=q_grp[:].rearrange("p q t -> p (q t)"),
+        )
+
+        pos_g = keep.tile([P, N], F32, name="pos_g")
+        nc.vector.tensor_copy(pos_g[:], pos_row[:].indirect(offsets[:]))
+        vs_g = keep.tile([P, N], F32, name="vs_g")
+        nc.vector.tensor_copy(vs_g[:], vs_row[:].indirect(offsets[:]))
+
+        cols = {}
+        for what, src in (("pos", pos_g), ("vs", vs_g)):
+            col = keep.tile([P, 2, 1, 4], F32, name=f"{what}_col")
+            for g in range(2):
+                turned = banks.tile([P, 4, P], F32, name="turned", tag="head", bufs=2)
+                for t in range(4):
+                    nc.tensor.transpose(turned[:, t, :], src[:, g * HALF + t : (g + 1) * HALF : 4], ident[:])
+                nc.vector.tensor_copy(col[:, g, 0, :], turned[:, :, 0])
+            cols[what] = col
+        bias = keep.tile([P, 2, 4, P], F32, name="bias")
+        for g in range(2):
+            spread = banks.tile([P, 4, P], F32, name="spread", tag="head", bufs=2)
+            for t in range(4):
+                nc.tensor.transpose(
+                    spread[:, t, :], cols["pos"][:, g, 0, t : t + 1].to_broadcast([P, P]), ident[:]
+                )
+            nc.scalar.activation(bias[:, g], spread[:], ACT.Copy, scale=slope_sb[:])
+
+        k_grp = keep.tile([P, N, 4], BF16, name="k_grp", align_bytes=64)
+        for t in range(3):
+            nc.vector.tensor_copy(k_grp[:, :, t], kp[t][:].indirect(offsets[:]))
+        for h in range(2):
+            nc.vector.tensor_copy(
+                k_grp[:, h * HALF : (h + 1) * HALF, 3],
+                kp[3][:, : (FIRST, T)[h]].indirect(offsets[:, h * 32 : (h + 1) * 32]),
+            )
+        k_codes = keep.tile([P, N], U32, name="k_codes", align_bytes=64)
+        k_scales = keep.tile([P, N], U8, name="k_scales", align_bytes=64)
+        score = []
+        for h in range(2):
+            c = slice(h * HALF, (h + 1) * HALF)
+            nc.vector.quantize_mx(
+                out=k_codes[:, c].bitcast(FP8X4),
+                scales=k_scales[:, c],
+                in_=k_grp[:, c, :].rearrange("p n t -> p (n t)"),
+            )
+            s_ps = banks.tile([P, HALF], F32, name=f"s_ps{h}")
+            nc.tensor.matmul_mx(
+                out=s_ps[:],
+                lhsT=q_codes[:].bitcast(FP8X4),
+                lhsT_scale=q_scales[:],
+                rhs=k_codes[:, c].bitcast(FP8X4),
+                rhs_scale=k_scales[:, c],
+                start=True,
+                stop=True,
+            )
+            score.append(s_ps)
+
+        s_sb = keep.tile([P, 2, 4, P], F32, name="s_sb")
+        for h in range(2):
+            nc.vector.tensor_tensor(
+                s_sb[:, h], score[h][:].rearrange("q (p t) -> q t p", t=4), bias[:, h], ALU.add
+            )
+        neg_max = keep.tile([P, 1], F32, name="neg_max")
+        nc.vector.tensor_reduce(
+            neg_max[:], s_sb[:].rearrange("q h t p -> q (h t p)"), AX.X, ALU.max, negate=True
+        )
+        prob = keep.tile([P, 2, 4, P], F32, name="prob")
+        sums = keep.tile([P, 2], F32, name="sums")
+        for h in range(2):
+            nc.scalar.activation(
+                prob[:, h], s_sb[:, h], ACT.Exp, bias=neg_max[:], accum_out=sums[:, h : h + 1]
+            )
+
+        w_codes = keep.tile([P, 2, P], U32, name="w_codes", align_bytes=64)
+        w_scales = keep.tile([P, 2, P], U8, name="w_scales", align_bytes=64)
+        v_codes = [keep.tile([P, 2, P], U32, name=f"v_codes{e}", align_bytes=64) for e in range(2)]
+        v_scales = [keep.tile([P, 2, P], U8, name=f"v_scales{e}", align_bytes=64) for e in range(2)]
+        v_g = [keep.tile([P, 2, 4, P], BF16, name=f"v_g{e}") for e in range(2)]
+        v_grp = [keep.tile([P, 2, P, 4], BF16, name=f"v_grp{e}", align_bytes=64) for e in range(2)]
+        w_grp = keep.tile([P, 2, P, 4], BF16, name="w_grp", align_bytes=64)
+
+        def gather_values(e, g):
+            nc.vector.tensor_copy(
+                v_g[e][:, g].rearrange("p t m -> p m t"),
+                vp[e][:, : (FIRST, T)[g]].indirect(offsets[:, g * 32 : (g + 1) * 32]),
+            )
+
+        def turn_values(e, g):
+            v_ps = banks.tile([P, 4, P], BF16, name="v_ps", tag="turn", bufs=4)
+            for t in range(4):
+                nc.tensor.transpose(v_ps[:, t, :], v_g[e][:, g, t, :], ident_b[:])
+            nc.scalar.copy(v_grp[e][:, g], v_ps[:].rearrange("p t e -> p e t"))
+
+        def quantise(codes, scales, grouped):
+            nc.vector.quantize_mx(out=codes.bitcast(FP8X4), scales=scales, in_=grouped)
+
+        gather_values(0, 0)
+        gather_values(0, 1)
+        total = keep.tile([P, 1], F32, name="total")
+        nc.vector.tensor_tensor(total[:], sums[:, 0:1], sums[:, 1:2], ALU.add)
+        inv = keep.tile([P, 1], F32, name="inv")
+        nc.vector.reciprocal(inv[:], total[:])
+        for g in range(2):
+            p_ps = banks.tile([P, 4, P], F32, name="p_ps", tag="turn", bufs=4)
+            for t in range(4):
+                nc.tensor.transpose(p_ps[:, t, :], prob[:, g, t, :], ident[:])
+            nc.vector.tensor_tensor(
+                w_grp[:, g],
+                p_ps[:].rearrange("p t q -> p q t"),
+                cols["vs"][:, g].to_broadcast([P, P, 4]),
+                ALU.mult,
+            )
+        turn_values(0, 0)
+        turn_values(0, 1)
+        for g in range(2):
+            quantise(w_codes[:, g], w_scales[:, g], w_grp[:, g].rearrange("p q t -> p (q t)"))
+        gather_values(1, 0)
+        gather_values(1, 1)
+        quantise(
+            v_codes[0][:].rearrange("p g e -> p (g e)"),
+            v_scales[0][:].rearrange("p g e -> p (g e)"),
+            v_grp[0][:].rearrange("p g e t -> p (g e t)"),
+        )
+        for g in range(2):
+            turn_values(1, g)
+            quantise(v_codes[1][:, g], v_scales[1][:, g], v_grp[1][:, g].rearrange("p e t -> p (e t)"))
+
+        y_sb = keep.tile([P, DV], F32, name="y_sb")
+        y_ps = banks.tile([P, DV], F32, name="y_ps", tag="head", bufs=2)
+        for e in range(2):
+            for g in range(2):
+                nc.tensor.matmul_mx(
+                    out=y_ps[:, e * P : (e + 1) * P],
+                    lhsT=w_codes[:, g].bitcast(FP8X4),
+                    lhsT_scale=w_scales[:, g],
+                    rhs=v_codes[e][:, g].bitcast(FP8X4),
+                    rhs_scale=v_scales[e][:, g],
+                    start=(g == 0),
+                    stop=(g == 1),
+                )
+        nc.vector.scalar_tensor_tensor(y_sb[:], y_ps[:], inv[:], gate[:], ALU.mult, ALU.mult)
+        nc.sync.dma_start(out[0], y_sb[:])

@@ -108,8 +108,13 @@ def tile_attend_x_alibi_gate_srt_kernel(tc, qT, kT, vT, vs, pos, slope, og, offs
             nc.scalar.activation(bias[:, g], spread[:], ACT.Copy, scale=slope_sb[:])
 
         k_grp = keep.tile([P, N, 4], BF16, name="k_grp", align_bytes=64)
-        for t in range(3):
-            nc.vector.tensor_copy(k_grp[:, :, t], kp[t][:].indirect(offsets[:]))
+        k_pair = keep.tile([P, 2, N], F32, name="k_pair")
+        for t in range(2):
+            nc.vector.tensor_copy(k_pair[:, t, :], kp[t][:].indirect(offsets[:]))
+        for h in range(2):
+            c = slice(h * HALF, (h + 1) * HALF)
+            nc.scalar.activation(k_grp[:, c, 0:2], k_pair[:, :, c].rearrange("p t n -> p n t"), ACT.Copy)
+        nc.vector.tensor_copy(k_grp[:, :, 2], kp[2][:].indirect(offsets[:]))
         for h in range(2):
             nc.vector.tensor_copy(
                 k_grp[:, h * HALF : (h + 1) * HALF, 3],

from contextlib import ExitStack

import concourse.mybir as mybir
from concourse.masks import make_identity

F32 = mybir.dt.float32
BF16 = mybir.dt.bfloat16
U32 = mybir.dt.uint32
U16 = mybir.dt.uint16
U8 = mybir.dt.uint8
FP8X4 = mybir.dt.float8_e4m3fn_x4
ACT = mybir.ActivationFunctionType
ALU = mybir.AluOpType
AX = mybir.AxisListType

P = 128
D = 512
DV = 256
T = 4096
N = 1024
HALF = 512
FIRST = T - HALF
FLOPS = 2 * N * D * P + 2 * N * P * DV
BYTES = 4 * (D * P + D * T + DV * T + 2 * T + P + 2 * P * DV) + 2 * P * (N // 16)


def tile_attend_x_alibi_gate_srt_kernel(tc, qT, kT, vT, vs, pos, slope, og, offs, out):
    nc = tc.nc
    with ExitStack() as ctx:
        keep = ctx.enter_context(tc.tile_pool(name="keep", bufs=1))
        banks = ctx.enter_context(tc.psum_pool(name="banks", bufs=1))

        offsets = keep.tile([P, N // 16], U16, name="offsets")
        nc.sync.dma_start(offsets[:], offs)

        pos_row = keep.tile([P, T], F32, name="pos_row")
        vs_row = keep.tile([P, T], F32, name="vs_row")
        kp = [keep.tile([P, T], F32, name=f"k_plane{t}") for t in range(4)]
        vp = [keep.tile([P, T], F32, name=f"v_plane{e}") for e in range(2)]
        k_planes = kT.rearrange("(p t) n -> p t n", t=4)

        nc.vector.memset(pos_row[:], 0.0)
        nc.gpsimd.memset(vs_row[:], 0.0)
        nc.vector.memset(kp[0][:, T // 2 : T // 2 + 8], 0.0)
        for plane in (kp[1], kp[2], kp[3], vp[0], vp[1]):
            nc.gpsimd.memset(plane[:, 0:8], 0.0)
        ident = keep.tile([P, P], F32, name="ident")
        make_identity(nc, ident[:])
        ident_b = keep.tile([P, P], BF16, name="ident_b")
        make_identity(nc, ident_b[:])

        q_raw = keep.tile([P, 4, P], F32, name="q_raw")
        nc.scalar.dma_start(q_raw[:], qT[0].rearrange("(p t) q -> p t q", t=4))
        og_sb = keep.tile([P, DV], F32, name="og_sb")
        nc.scalar.dma_start(og_sb[:], og[0])
        slope_sb = keep.tile([P, 1], F32, name="slope_sb")
        nc.scalar.dma_start(slope_sb[:], slope[0])
        nc.sync.dma_start(kp[0][:, : T // 2], k_planes[:, 0, : T // 2])
        nc.sync.dma_start(pos_row[0:1, :], pos[0:1, :])
        nc.sync.dma_start(kp[0][:, T // 2 :], k_planes[:, 0, T // 2 :])
        nc.sync.dma_start(vs_row[0:1, :], vs[0:1, :])
        for t in range(1, 4):
            if t < 3:
                nc.sync.dma_start(kp[t][:], k_planes[:, t, :])
            else:
                nc.sync.dma_start(kp[t][:, :FIRST], k_planes[:, t, :FIRST])
                nc.sync.dma_start(kp[t][:, FIRST:], k_planes[:, t, FIRST:])
        nc.sync.dma_start(vp[0][:], vT[0:P, :])
        nc.sync.dma_start(vp[1][:, :FIRST], vT[P : 2 * P, :FIRST])
        nc.sync.dma_start(vp[1][:, FIRST:], vT[P : 2 * P, FIRST:])

        gate = keep.tile([P, DV], F32, name="gate")
        nc.scalar.activation(gate[:], og_sb[:], ACT.Sigmoid)
        warm = keep.tile([P, 1], F32, name="warm")
        nc.scalar.activation(warm[:], slope_sb[:], ACT.Exp)

        q_grp = keep.tile([P, P, 4], BF16, name="q_grp", align_bytes=64)
        nc.scalar.copy(q_grp[:], q_raw[:].rearrange("p t q -> p q t"))
        q_codes = keep.tile([P, P], U32, name="q_codes", align_bytes=64)
        q_scales = keep.tile([P, P], U8, name="q_scales", align_bytes=64)
        nc.vector.quantize_mx(
            out=q_codes[:].bitcast(FP8X4),
            scales=q_scales[:],
            in_=q_grp[:].rearrange("p q t -> p (q t)"),
        )

        pos_g = keep.tile([P, N], F32, name="pos_g")
        nc.vector.tensor_copy(pos_g[:], pos_row[:].indirect(offsets[:]))
        vs_g = keep.tile([P, N], F32, name="vs_g")
        nc.vector.tensor_copy(vs_g[:], vs_row[:].indirect(offsets[:]))

        cols = {}
        for what, src in (("pos", pos_g), ("vs", vs_g)):
            col = keep.tile([P, 2, 1, 4], F32, name=f"{what}_col")
            for g in range(2):
                turned = banks.tile([P, 4, P], F32, name="turned", tag="head", bufs=2)
                for t in range(4):
                    nc.tensor.transpose(turned[:, t, :], src[:, g * HALF + t : (g + 1) * HALF : 4], ident[:])
                nc.vector.tensor_copy(col[:, g, 0, :], turned[:, :, 0])
            cols[what] = col
        bias = keep.tile([P, 2, 4, P], F32, name="bias")
        for g in range(2):
            spread = banks.tile([P, 4, P], F32, name="spread", tag="head", bufs=2)
            for t in range(4):
                nc.tensor.transpose(
                    spread[:, t, :], cols["pos"][:, g, 0, t : t + 1].to_broadcast([P, P]), ident[:]
                )
            nc.scalar.activation(bias[:, g], spread[:], ACT.Copy, scale=slope_sb[:])

        k_grp = keep.tile([P, N, 4], BF16, name="k_grp", align_bytes=64)
        k_pair = keep.tile([P, 2, N], F32, name="k_pair")
        for t in range(2):
            nc.vector.tensor_copy(k_pair[:, t, :], kp[t][:].indirect(offsets[:]))
        for h in range(2):
            c = slice(h * HALF, (h + 1) * HALF)
            nc.scalar.activation(k_grp[:, c, 0:2], k_pair[:, :, c].rearrange("p t n -> p n t"), ACT.Copy)
        nc.vector.tensor_copy(k_grp[:, :, 2], kp[2][:].indirect(offsets[:]))
        for h in range(2):
            nc.vector.tensor_copy(
                k_grp[:, h * HALF : (h + 1) * HALF, 3],
                kp[3][:, : (FIRST, T)[h]].indirect(offsets[:, h * 32 : (h + 1) * 32]),
            )
        k_codes = keep.tile([P, N], U32, name="k_codes", align_bytes=64)
        k_scales = keep.tile([P, N], U8, name="k_scales", align_bytes=64)
        score = []
        for h in range(2):
            c = slice(h * HALF, (h + 1) * HALF)
            nc.vector.quantize_mx(
                out=k_codes[:, c].bitcast(FP8X4),
                scales=k_scales[:, c],
                in_=k_grp[:, c, :].rearrange("p n t -> p (n t)"),
            )
            s_ps = banks.tile([P, HALF], F32, name=f"s_ps{h}")
            nc.tensor.matmul_mx(
                out=s_ps[:],
                lhsT=q_codes[:].bitcast(FP8X4),
                lhsT_scale=q_scales[:],
                rhs=k_codes[:, c].bitcast(FP8X4),
                rhs_scale=k_scales[:, c],
                start=True,
                stop=True,
            )
            score.append(s_ps)

        s_sb = keep.tile([P, 2, 4, P], F32, name="s_sb")
        for h in range(2):
            nc.vector.tensor_tensor(
                s_sb[:, h], score[h][:].rearrange("q (p t) -> q t p", t=4), bias[:, h], ALU.add
            )
        neg_max = keep.tile([P, 1], F32, name="neg_max")
        nc.vector.tensor_reduce(
            neg_max[:], s_sb[:].rearrange("q h t p -> q (h t p)"), AX.X, ALU.max, negate=True
        )
        prob = keep.tile([P, 2, 4, P], F32, name="prob")
        sums = keep.tile([P, 2], F32, name="sums")
        for h in range(2):
            nc.scalar.activation(
                prob[:, h], s_sb[:, h], ACT.Exp, bias=neg_max[:], accum_out=sums[:, h : h + 1]
            )

        w_codes = keep.tile([P, 2, P], U32, name="w_codes", align_bytes=64)
        w_scales = keep.tile([P, 2, P], U8, name="w_scales", align_bytes=64)
        v_codes = [keep.tile([P, 2, P], U32, name=f"v_codes{e}", align_bytes=64) for e in range(2)]
        v_scales = [keep.tile([P, 2, P], U8, name=f"v_scales{e}", align_bytes=64) for e in range(2)]
        v_g = [keep.tile([P, 2, 4, P], BF16, name=f"v_g{e}") for e in range(2)]
        v_grp = [keep.tile([P, 2, P, 4], BF16, name=f"v_grp{e}", align_bytes=64) for e in range(2)]
        w_grp = keep.tile([P, 2, P, 4], BF16, name="w_grp", align_bytes=64)

        def gather_values(e, g):
            nc.vector.tensor_copy(
                v_g[e][:, g].rearrange("p t m -> p m t"),
                vp[e][:, : (FIRST, T)[g]].indirect(offsets[:, g * 32 : (g + 1) * 32]),
            )

        def turn_values(e, g):
            v_ps = banks.tile([P, 4, P], BF16, name="v_ps", tag="turn", bufs=4)
            for t in range(4):
                nc.tensor.transpose(v_ps[:, t, :], v_g[e][:, g, t, :], ident_b[:])
            nc.scalar.copy(v_grp[e][:, g], v_ps[:].rearrange("p t e -> p e t"))

        def quantise(codes, scales, grouped):
            nc.vector.quantize_mx(out=codes.bitcast(FP8X4), scales=scales, in_=grouped)

        gather_values(0, 0)
        gather_values(0, 1)
        total = keep.tile([P, 1], F32, name="total")
        nc.vector.tensor_tensor(total[:], sums[:, 0:1], sums[:, 1:2], ALU.add)
        inv = keep.tile([P, 1], F32, name="inv")
        nc.vector.reciprocal(inv[:], total[:])
        for g in range(2):
            p_ps = banks.tile([P, 4, P], F32, name="p_ps", tag="turn", bufs=4)
            for t in range(4):
                nc.tensor.transpose(p_ps[:, t, :], prob[:, g, t, :], ident[:])
            nc.vector.tensor_tensor(
                w_grp[:, g],
                p_ps[:].rearrange("p t q -> p q t"),
                cols["vs"][:, g].to_broadcast([P, P, 4]),
                ALU.mult,
            )
        turn_values(0, 0)
        turn_values(0, 1)
        for g in range(2):
            quantise(w_codes[:, g], w_scales[:, g], w_grp[:, g].rearrange("p q t -> p (q t)"))
        gather_values(1, 0)
        gather_values(1, 1)
        quantise(
            v_codes[0][:].rearrange("p g e -> p (g e)"),
            v_scales[0][:].rearrange("p g e -> p (g e)"),
            v_grp[0][:].rearrange("p g e t -> p (g e t)"),
        )
        for g in range(2):
            turn_values(1, g)
            quantise(v_codes[1][:, g], v_scales[1][:, g], v_grp[1][:, g].rearrange("p e t -> p (e t)"))

        y_sb = keep.tile([P, DV], F32, name="y_sb")
        y_ps = banks.tile([P, DV], F32, name="y_ps", tag="head", bufs=2)
        for e in range(2):
            for g in range(2):
                nc.tensor.matmul_mx(
                    out=y_ps[:, e * P : (e + 1) * P],
                    lhsT=w_codes[:, g].bitcast(FP8X4),
                    lhsT_scale=w_scales[:, g],
                    rhs=v_codes[e][:, g].bitcast(FP8X4),
                    rhs_scale=v_scales[e][:, g],
                    start=(g == 0),
                    stop=(g == 1),
                )
        nc.vector.scalar_tensor_tensor(y_sb[:], y_ps[:], inv[:], gate[:], ALU.mult, ALU.mult)
        nc.sync.dma_start(out[0], y_sb[:])
